import numpy as np
import ml_dtypes


def mxq(x, axis, fmt="e4m3"):
    dtype, down = {"e4m3": (ml_dtypes.float8_e4m3fn, 7), "e5m2": (ml_dtypes.float8_e5m2, 14)}[fmt]
    v = np.moveaxis(np.asarray(x, np.float32).astype(ml_dtypes.bfloat16).astype(np.float64), axis, -1)
    blocks = v.reshape(v.shape[:-1] + (-1, 32))
    amax = np.abs(blocks).max(-1, keepdims=True)
    byte = np.maximum(np.where(amax > 0, np.frexp(amax)[1] - 1 + 127, 0) - down, 1)
    scale = np.exp2(byte - 127.0)
    codes = (blocks / scale).astype(np.float32).astype(dtype).astype(np.float64)
    return np.moveaxis((codes * scale).reshape(v.shape), -1, axis)


WIDE = False


def mx_kscale(k):
    if not WIDE:
        return np.ones(k)
    levels = np.array([10, -10, 5, -5, 0])
    if k % 512:
        return np.exp2(np.random.permutation(np.resize(levels, k // 32))).repeat(32)
    a = np.empty((k // 512, 16))
    for p in range(k // 512):
        a[p, :8] = np.random.permutation(np.resize(levels, 8))
        for g in range(8):
            far = levels[np.abs(levels - a[p, g]) >= 10]
            a[p, g + 8] = far[np.random.randint(len(far))]
    return np.exp2(a.ravel()).repeat(32)


def f64(x):
    return np.asarray(x).astype(np.float64)


def striped(idx):
    return np.tile(np.asarray(idx).reshape(-1, 16).T, (8, 1)).astype(np.uint16)


def unstriped(offs):
    return offs[:16].T.reshape(-1).astype(np.int64)


E2M1 = np.array([0.0, 0.5, 1.0, 1.5, 2.0, 3.0, 4.0, 6.0, -0.0, -0.5, -1.0, -1.5, -2.0, -3.0, -4.0, -6.0])


def pack_weight(w, fmt):
    k, n = w.shape
    w = f64(np.asarray(w, np.float32).astype(ml_dtypes.bfloat16)).reshape(k // 32, 32, n)
    amax = np.abs(w).max(1)
    if fmt == "e4m3":
        byte = np.frexp(amax)[1] - 1 + 127 - 7
    else:
        mant, ex = np.frexp(amax / 6.0)
        byte = np.where(mant > 0.5, ex, ex - 1) + 127
    byte = np.clip(np.where(amax > 0, byte, 1), 1, 254)
    scaled = (w * np.exp2(127.0 - byte)[:, None, :]).reshape(k, n).astype(np.float32)
    by_word = np.ascontiguousarray(scaled.reshape(k // 512, 128, 4, n).transpose(0, 1, 3, 2))
    if fmt == "e4m3":
        words = by_word.astype(ml_dtypes.float8_e4m3fn).view(np.uint8)
    else:
        c = by_word.astype(ml_dtypes.float4_e2m1fn).view(np.uint8) & 0xF
        words = (c[..., 0::2] | (c[..., 1::2] << 4)).reshape(k // 512, 128, 2 * n)
    return np.ascontiguousarray(words), np.ascontiguousarray(byte.astype(np.uint8).reshape(k // 512, 16, n))


def unpack_weight(words, scales, fmt):
    g, _, n = scales.shape
    words = np.ascontiguousarray(words).reshape(g, 128, n, -1)
    if fmt == "e4m3":
        vals = words.view(ml_dtypes.float8_e4m3fn).astype(np.float64)
    else:
        nib = np.empty((g, 128, n, 4), np.uint8)
        nib[..., 0::2] = words & 0xF
        nib[..., 1::2] = words >> 4
        vals = E2M1[nib]
    vals = vals * np.repeat(np.exp2(scales.astype(np.float64) - 127.0), 8, axis=1)[..., None]
    return vals.transpose(0, 1, 3, 2).reshape(g * 512, n)


def sigmoid(v):
    return 1.0 / (1.0 + np.exp(-v))


D, E, T, I, Q, G = 512, 512, 2048, 512, 128, 32


def setup_inputs():
    n = np.random.standard_normal
    idx = np.random.permutation(T)[:I]
    fd = mx_kscale(D)
    fe = mx_kscale(E)
    keysp = pack_weight(n((D, T)) / fd[:, None], "e4m3")
    valsp = pack_weight(n((E, T)) / fe[:, None], "e4m3")
    return {
        "query": (n((D, Q)) * 0.7 / np.sqrt(D) * fd[:, None]).astype(np.float32),
        "keys_words": keysp[0],
        "keys_scales": keysp[1],
        "th": (np.random.uniform(-0.2, 0.2, (Q, 1))).astype(np.float32),
        "steep": (np.random.uniform(2.0, 8.0, (Q, 1))).astype(np.float32),
        "gout": (n((E, Q)) * 1 / np.sqrt(E) * fe[:, None]).astype(np.float32),
        "vals_words": valsp[0],
        "vals_scales": valsp[1],
        "size": (np.random.uniform(0.5, 2.0, (1, I))).astype(np.float32),
        "dquery": (n((D, Q)) * 1.0 / np.sqrt(D) * fd[:, None]).astype(np.float32),
        "base": (0.5 * n((Q, T))).astype(np.float32),
        "offs": striped(idx),
    }


def reference(query, keys_words, keys_scales, th, steep, gout, vals_words, vals_scales, size, dquery, base, offs):
    idx = unstriped(offs)
    keysu = unpack_weight(keys_words, keys_scales, "e4m3")
    valsu = unpack_weight(vals_words, vals_scales, "e4m3")
    queryq = mxq(f64(query), 0, "e4m3")
    keysidxg = keysu[:, idx]
    a = queryq.T @ keysidxg
    dqueryq = mxq(f64(dquery), 0, "e4m3")
    ta = dqueryq.T @ keysidxg
    s = a.reshape(Q, G, I // G).mean(axis=2)
    gt = sigmoid((s - f64(th)) * f64(steep))
    gr = np.repeat(gt, I // G, axis=1)
    r = np.exp(a - np.max(a, axis=1, keepdims=True))
    p = r * gr
    z = np.sum(p, axis=1, keepdims=True)
    goutq = mxq(f64(gout), 0, "e4m3")
    valsidxg = valsu[:, idx]
    c0 = goutq.T @ valsidxg
    dz = np.sum(c0 * p * f64(size) / np.square(z) * (-1.0), axis=1, keepdims=True)
    dp = c0 / z * f64(size) + dz
    dr = dp * gr
    dgr = dp * r
    dgt = dgr.reshape(Q, G, I // G).sum(axis=2)
    ts = ta.reshape(Q, G, I // G).mean(axis=2)
    tgt = ts * f64(steep) * gt * (1.0 - gt)
    tgr = np.repeat(tgt, I // G, axis=1)
    tr = ta * r
    tp = tr * gr + tgr * r
    tz = np.sum(tp, axis=1, keepdims=True)
    tdz = np.sum((tp * f64(size) * c0 - tz * z * 2.0 * c0 * p * f64(size) / np.square(z)) / np.square(z) * (-1.0), axis=1, keepdims=True)
    tdp = tz * c0 / np.square(z) * (-1.0) * f64(size) + tdz
    tdr = tdp * gr + tgr * dp
    tdgr = tdp * r + tr * dp
    tdgt = tdgr.reshape(Q, G, I // G).sum(axis=2)
    tds = ((tdgt * gt + tgt * dgt) * (1.0 - gt) + tgt * (-1.0) * dgt * gt) * f64(steep)
    te1 = tds / 16.0
    tr1 = np.repeat(te1, I // G, axis=1)
    tda = tdr * r + tr * dr + tr1
    gs = tda * 512.0
    gf = np.zeros((Q, T))
    gf[:, idx] = gs
    y = f64(base) + gf
    return y

@@ -1,0 +1,225 @@
+from contextlib import ExitStack
+
+import concourse.mybir as mybir
+from concourse.masks import make_identity
+
+D, E, T, I, Q, G = 512, 512, 2048, 512, 128, 32
+P = 128
+PACK = 4
+PAGE = I // G
+HALF = I // 2
+FLOPS = 3 * 2 * D * Q * I
+
+F32 = mybir.dt.float32
+BF16 = mybir.dt.bfloat16
+I32 = mybir.dt.int32
+U32 = mybir.dt.uint32
+U16 = mybir.dt.uint16
+U8 = mybir.dt.uint8
+FP8X4 = mybir.dt.float8_e4m3fn_x4
+ALU = mybir.AluOpType
+ACT = mybir.ActivationFunctionType
+AX = mybir.AxisListType
+
+VAL_PLANE = 4
+SCATTERS = 4
+STORES = 4
+
+
+def paged(ap):
+    return ap.rearrange("p (g j) -> p g j", j=PAGE)
+
+
+def over_page(ap):
+    return ap.unsqueeze(2).to_broadcast([P, ap.shape[1], PAGE])
+
+
+def tile_attend_hvpagegate_s_kernel(tc, query, keys_words, keys_scales, th, steep, gout, vals_words, vals_scales,
+                                     size, dquery, base, offs, out):
+    nc = tc.nc
+    with ExitStack() as ctx:
+        held = ctx.enter_context(tc.tile_pool(name="held", bufs=1))
+        sb = ctx.enter_context(tc.tile_pool(name="sb", bufs=1))
+        ps = ctx.enter_context(tc.psum_pool(name="ps", bufs=1))
+
+        offsets = held.tile([P, I // 16], U16, name="offsets")
+        nc.sync.dma_start(offsets[:], offs)
+
+        def load_rows(src, name):
+            raw = sb.tile([P, PACK, Q], F32, name=name, tag="raw")
+            nc.sync.dma_start(out=raw[:], in_=src.rearrange("(p j) w -> p j w", j=PACK))
+            return raw
+
+        def round_rows(raw, name):
+            grouped = sb.tile([P, Q, PACK], BF16, name=name, tag=name, align_bytes=64)
+            nc.scalar.copy(out=grouped[:], in_=raw[:].rearrange("p j w -> p w j"))
+            return grouped
+
+        def quantize(grouped, name):
+            codes = sb.tile([P, Q], U32, name=name + "_codes", align_bytes=64)
+            scales = sb.tile([P, Q], U8, name=name + "_scales", align_bytes=64)
+            nc.vector.quantize_mx(out=codes[:].bitcast(FP8X4), scales=scales[:],
+                                  in_=grouped[:].rearrange("p w j -> p (w j)"))
+            return codes, scales
+
+        def load_words(words, name, tag):
+            window = sb.tile([P, T], U32, name=name, tag=tag)
+            nc.sync.dma_start(out=window[:].bitcast(I32), in_=words[0].rearrange("p n t -> p (n t)").bitcast(I32))
+            return window
+
+        def load_scale_rows(window, scales, first, queues):
+            for quad, queue in enumerate(queues):
+                row = 32 * quad + first
+                queue.dma_start(out=window[row:row + 4, :].bitcast(I32),
+                                in_=scales[0, 4 * quad:4 * quad + 4, :].bitcast(I32))
+
+        key_scale_pool = sb.tile([P, T], U8, name="key_scale_pool", tag="second")
+        val_scale_pool = sb.tile([P, T], U8, name="val_scale_pool")
+        nc.vector.memset(key_scale_pool[:].bitcast(I32), 0)
+        nc.vector.memset(val_scale_pool[:].bitcast(I32), 0)
+        q_raw = load_rows(query, "q_raw")
+        key_pool = load_words(keys_words, "key_pool", "first")
+        load_scale_rows(key_scale_pool, keys_scales, 0, [nc.scalar] * 4)
+        load_scale_rows(val_scale_pool, vals_scales, VAL_PLANE, [nc.scalar] * 3 + [nc.gpsimd])
+        th_col = sb.tile([P, 1], F32, name="th_col")
+        steep_col = sb.tile([P, 1], F32, name="steep_col")
+        nc.gpsimd.dma_start(out=steep_col[:], in_=steep)
+        nc.gpsimd.dma_start(out=th_col[:], in_=th)
+        ident = sb.tile([P, P], F32, name="ident")
+        make_identity(nc, ident[:])
+        placed = sb.tile([P, T], F32, name="placed")
+        nc.vector.memset(placed[:], 0.0)
+
+        key_scales = sb.tile([P, I], U8, name="key_scales", align_bytes=64)
+        nc.vector.tensor_copy(key_scales[:], key_scale_pool[:].indirect(offsets[:]))
+        q_bf = round_rows(q_raw, "q_bf")
+        warm = sb.tile([P, 1], F32, name="warm")
+        nc.scalar.activation(warm[:], q_bf[:, 0, 0:1], ACT.Exp, scale=0.0)
+        dq_raw = load_rows(dquery, "dq_raw")
+        val_pool = load_words(vals_words, "val_pool", "second")
+        q_codes, q_scales = quantize(q_bf, "q")
+        size_cols = sb.tile([P, I // P], F32, name="size_cols", tag="q_bf", align_bytes=64)
+        with nc.allow_non_contiguous_dma(reason="one weight a partition"):
+            nc.sync.dma_start(out=size_cols[:], in_=size[0].rearrange("(t p) -> p t", p=P))
+        val_scales = sb.tile([P, I], U8, name="val_scales", align_bytes=64)
+        nc.vector.tensor_copy(val_scales[:], val_scale_pool[:].indirect(offsets[:]))
+
+        neg_slope = sb.tile([P, 1], F32, name="neg_slope")
+        slope = sb.tile([P, 1], F32, name="slope")
+        shift = sb.tile([P, 1], F32, name="shift")
+        c_scale = sb.tile([P, I // P], F32, name="c_scale")
+        nc.gpsimd.tensor_scalar(neg_slope[:], steep_col[:], -1.0 / PAGE, 0.0, ALU.mult, ALU.add)
+        nc.gpsimd.tensor_scalar(slope[:], steep_col[:], 1.0 / PAGE, 0.0, ALU.mult, ALU.add)
+        nc.gpsimd.tensor_tensor(shift[:], steep_col[:], th_col[:], ALU.mult)
+        nc.gpsimd.tensor_scalar(c_scale[:], size_cols[:], -512.0, 0.0, ALU.mult, ALU.add)
+
+        halves = [slice(h * HALF, (h + 1) * HALF) for h in range(2)]
+        page_halves = [slice(h * G // 2, (h + 1) * G // 2) for h in range(2)]
+        key_words = sb.tile([P, I], U32, name="key_words", align_bytes=64)
+        a_ps = [ps.tile([P, HALF], F32, name="a_ps%d" % h) for h in range(2)]
+        for h in range(2):
+            nc.vector.tensor_copy(key_words[:, halves[h]], key_pool[:].indirect(offsets[:, page_halves[h]]))
+            nc.tensor.matmul_mx(out=a_ps[h][:], lhsT=q_codes[:].bitcast(FP8X4), lhsT_scale=q_scales[:],
+                                rhs=key_words[:, halves[h]].bitcast(FP8X4), rhs_scale=key_scales[:, halves[h]],
+                                start=True, stop=True)
+        dq_bf = round_rows(dq_raw, "dq_bf")
+        go_raw = load_rows(gout, "go_raw")
+
+        a_sum = sb.tile([P, G], F32, name="a_sum")
+        a_max = sb.tile([P, 2], F32, name="a_max")
+        neg_max = sb.tile([P, 1], F32, name="neg_max")
+        for h in range(2):
+            nc.vector.tensor_reduce(a_sum[:, page_halves[h]], paged(a_ps[h][:]), AX.X, ALU.add)
+            nc.vector.tensor_reduce(a_max[:, h:h + 1], a_ps[h][:], AX.X, ALU.max)
+        dq_codes, dq_scales = quantize(dq_bf, "dq")
+        nc.vector.tensor_reduce(neg_max[:], a_max[:], AX.X, ALU.max, negate=True)
+        ta_ps = ps.tile([P, I], F32, name="ta_ps")
+        nc.tensor.matmul_mx(out=ta_ps[:], lhsT=dq_codes[:].bitcast(FP8X4), lhsT_scale=dq_scales[:],
+                            rhs=key_words[:].bitcast(FP8X4), rhs_scale=key_scales[:], start=True, stop=True)
+
+        odds = sb.tile([P, G], F32, name="odds")
+        denom = sb.tile([P, G], F32, name="denom")
+        nc.scalar.activation(odds[:], a_sum[:], ACT.Exp, bias=shift[:], scale=neg_slope[:])
+        nc.scalar.activation(denom[:], odds[:], ACT.Identity, bias=1.0)
+        r = sb.tile([P, I], F32, name="r")
+        for h in range(2):
+            nc.scalar.activation(r[:, halves[h]], a_ps[h][:], ACT.Exp, bias=neg_max[:])
+        go_bf = round_rows(go_raw, "go_bf")
+
+        val_words = sb.tile([P, I], U32, name="val_words", align_bytes=64)
+        nc.vector.tensor_copy(val_words[:], val_pool[:].indirect(offsets[:]))
+        go_codes, go_scales = quantize(go_bf, "go")
+        base_sb = sb.tile([P, T], F32, name="base_sb", tag="second")
+        nc.sync.dma_start(out=base_sb[:], in_=base)
+        ct_ps = [ps.tile([P, 2, Q], F32, name="ct_ps%d" % h) for h in range(2)]
+        ct = sb.tile([P, I // P, Q], F32, name="ct")
+        c_ps = ps.tile([P, I], F32, name="c_ps")
+        for t in range(I // P):
+            cols = slice(t * P, (t + 1) * P)
+            nc.tensor.matmul_mx(out=ct_ps[t // 2][:, t % 2, :], lhsT=val_words[:, cols].bitcast(FP8X4),
+                                lhsT_scale=val_scales[VAL_PLANE:P, cols], rhs=go_codes[:].bitcast(FP8X4),
+                                rhs_scale=go_scales[:], start=True, stop=True)
+        for t in range(I // P):
+            nc.scalar.activation(ct[:, t, :], ct_ps[t // 2][:, t % 2, :], ACT.Copy, scale=c_scale[:, t:t + 1])
+        for t in range(I // P):
+            nc.tensor.transpose(c_ps[:, t * P:(t + 1) * P], ct[:, t, :], ident[:])
+
+        gate = sb.tile([P, G], F32, name="gate")
+        ta_sum = sb.tile([P, G], F32, name="ta_sum")
+        k_m = sb.tile([P, G], F32, name="k_m")
+        lift = sb.tile([P, G], F32, name="lift")
+        k_n = sb.tile([P, G], F32, name="k_n")
+        nc.vector.reciprocal(gate[:], denom[:])
+        nc.vector.tensor_reduce(ta_sum[:], paged(ta_ps[:]), AX.X, ALU.add)
+        nc.vector.tensor_scalar(k_m[:], gate[:], 1.0, neg_slope[:], ALU.subtract, ALU.mult)
+        p = sb.tile([P, I], F32, name="p")
+        z = sb.tile([P, 1], F32, name="z")
+        nc.vector.scalar_tensor_tensor(paged(p[:]), paged(r[:]), 1.0, over_page(gate[:]), ALU.mult, ALU.mult,
+                                       accum_out=z[:])
+        nc.vector.tensor_tensor(lift[:], ta_sum[:], k_m[:], ALU.mult)
+        inv_z = sb.tile([P, 1], F32, name="inv_z")
+        nc.vector.reciprocal(inv_z[:], z[:])
+        w = sb.tile([P, I], F32, name="w")
+        nc.vector.tensor_tensor(paged(w[:]), paged(ta_ps[:]), over_page(lift[:]), ALU.add)
+        prob = sb.tile([P, I], F32, name="prob")
+        nc.scalar.activation(prob[:], p[:], ACT.Copy, scale=inv_z[:])
+        nc.vector.scalar_tensor_tensor(k_n[:], lift[:], slope[:], gate[:], ALU.mult, ALU.mult)
+        terms = sb.tile([P, I], F32, name="terms")
+        terms2 = sb.tile([P, I], F32, name="terms2")
+        c_mean = sb.tile([P, 1], F32, name="c_mean")
+        w_mean = sb.tile([P, 1], F32, name="w_mean")
+        nc.vector.scalar_tensor_tensor(terms[:], c_ps[:], inv_z[:], p[:], ALU.mult, ALU.mult, accum_out=c_mean[:])
+        nc.vector.scalar_tensor_tensor(terms2[:], w[:], inv_z[:], p[:], ALU.mult, ALU.mult, accum_out=w_mean[:])
+        u = sb.tile([P, I], F32, name="u")
+        nc.vector.scalar_tensor_tensor(u[:], c_ps[:], c_mean[:], prob[:], ALU.subtract, ALU.mult)
+        v = sb.tile([P, I], F32, name="v")
+        cov = sb.tile([P, 1], F32, name="cov")
+        nc.vector.scalar_tensor_tensor(v[:], w[:], w_mean[:], u[:], ALU.subtract, ALU.mult, accum_out=cov[:])
+        u_sum = sb.tile([P, G], F32, name="u_sum")
+        nc.vector.tensor_reduce(u_sum[:], paged(u[:]), AX.X, ALU.add)
+        m = [sb.tile([P, HALF], F32, name="m%d" % h) for h in range(2)]
+        m_sum = [sb.tile([P, G // 2], F32, name="m_sum%d" % h) for h in range(2)]
+        n_term = sb.tile([P, G], F32, name="n_term")
+        for h in range(2):
+            nc.vector.scalar_tensor_tensor(m[h][:], prob[:, halves[h]], cov[:], v[:, halves[h]], ALU.mult,
+                                           ALU.subtract)
+        nc.vector.tensor_tensor(n_term[:], u_sum[:], k_n[:], ALU.mult)
+        for h in range(2):
+            nc.vector.tensor_reduce(m_sum[h][:], paged(m[h][:]), AX.X, ALU.add)
+        pages = G // SCATTERS
+        for s in range(SCATTERS):
+            spread = sb.tile([P, pages, PAGE], F32, name="spread%d" % s)
+            h, first = divmod(s * pages, G // 2)
+            for j in range(pages):
+                g = s * pages + j
+                nc.scalar.activation(spread[:, j, :], m_sum[h][:, first + j:first + j + 1].to_broadcast([P, PAGE]),
+                                     ACT.Identity, bias=n_term[:, g:g + 1], scale=k_m[:, g:g + 1])
+            nc.vector.tensor_tensor(placed[:].indirect(offsets[:, s * pages:(s + 1) * pages]),
+                                    m[h][:, first * PAGE:(first + pages) * PAGE],
+                                    spread[:].rearrange("p g j -> p (g j)"), ALU.add)
+        width = T // STORES
+        for s in range(STORES):
+            cols = slice(s * width, (s + 1) * width)
+            res = sb.tile([P, width], F32, name="res%d" % s)
+            nc.vector.tensor_tensor(res[:], placed[:, cols], base_sb[:, cols], ALU.add)
+            nc.sync.dma_start(out=out[:, cols], in_=res[:])

@@ -22,8 +22,8 @@ ACT = mybir.ActivationFunctionType
 AX = mybir.AxisListType
 
 VAL_PLANE = 4
-SCATTERS = 4
-STORES = 4
+SCATTERS = ((0, 8), (8, 16), (16, 32))
+STORES = (256, 512, 512, 512, 256)
 
 
 def paged(ap):
@@ -40,20 +40,18 @@ def tile_attend_hvpagegate_s_kernel(tc, query, keys_words, keys_scales, th, stee
     with ExitStack() as ctx:
         held = ctx.enter_context(tc.tile_pool(name="held", bufs=1))
         sb = ctx.enter_context(tc.tile_pool(name="sb", bufs=1))
+        stage = ctx.enter_context(tc.tile_pool(name="stage", bufs=1))
+        early = ctx.enter_context(tc.tile_pool(name="early", bufs=1))
         ps = ctx.enter_context(tc.psum_pool(name="ps", bufs=1))
 
         offsets = held.tile([P, I // 16], U16, name="offsets")
         nc.sync.dma_start(offsets[:], offs)
 
-        def load_rows(src, name):
-            raw = sb.tile([P, PACK, Q], F32, name=name, tag="raw")
+        def load_rows(src, raw):
             nc.sync.dma_start(out=raw[:], in_=src.rearrange("(p j) w -> p j w", j=PACK))
-            return raw
 
-        def round_rows(raw, name):
-            grouped = sb.tile([P, Q, PACK], BF16, name=name, tag=name, align_bytes=64)
+        def round_rows(raw, grouped):
             nc.scalar.copy(out=grouped[:], in_=raw[:].rearrange("p j w -> p w j"))
-            return grouped
 
         def quantize(grouped, name):
             codes = sb.tile([P, Q], U32, name=name + "_codes", align_bytes=64)
@@ -62,10 +60,8 @@ def tile_attend_hvpagegate_s_kernel(tc, query, keys_words, keys_scales, th, stee
                                   in_=grouped[:].rearrange("p w j -> p (w j)"))
             return codes, scales
 
-        def load_words(words, name, tag):
-            window = sb.tile([P, T], U32, name=name, tag=tag)
+        def load_words(words, window):
             nc.sync.dma_start(out=window[:].bitcast(I32), in_=words[0].rearrange("p n t -> p (n t)").bitcast(I32))
-            return window
 
         def load_scale_rows(window, scales, first, queues):
             for quad, queue in enumerate(queues):
@@ -73,45 +69,43 @@ def tile_attend_hvpagegate_s_kernel(tc, query, keys_words, keys_scales, th, stee
                 queue.dma_start(out=window[row:row + 4, :].bitcast(I32),
                                 in_=scales[0, 4 * quad:4 * quad + 4, :].bitcast(I32))
 
-        key_scale_pool = sb.tile([P, T], U8, name="key_scale_pool", tag="second")
-        val_scale_pool = sb.tile([P, T], U8, name="val_scale_pool")
-        nc.vector.memset(key_scale_pool[:].bitcast(I32), 0)
-        nc.vector.memset(val_scale_pool[:].bitcast(I32), 0)
-        q_raw = load_rows(query, "q_raw")
-        key_pool = load_words(keys_words, "key_pool", "first")
-        load_scale_rows(key_scale_pool, keys_scales, 0, [nc.scalar] * 4)
-        load_scale_rows(val_scale_pool, vals_scales, VAL_PLANE, [nc.scalar] * 3 + [nc.gpsimd])
+        key_scale_pool = sb.tile([P, T], U8, name="key_scale_pool")
+        q_raw = stage.tile([P, PACK, Q], F32, name="q_raw", offset=2016)
+        load_rows(query, q_raw)
         th_col = sb.tile([P, 1], F32, name="th_col")
         steep_col = sb.tile([P, 1], F32, name="steep_col")
-        nc.gpsimd.dma_start(out=steep_col[:], in_=steep)
-        nc.gpsimd.dma_start(out=th_col[:], in_=th)
+        nc.sync.dma_start(out=steep_col[:], in_=steep)
+        nc.sync.dma_start(out=th_col[:], in_=th)
+        key_pool = sb.tile([P, T], U32, name="key_pool")
+        load_words(keys_words, key_pool)
+        nc.gpsimd.memset(key_scale_pool[:].bitcast(I32), 0)
+        load_scale_rows(key_scale_pool, keys_scales, 0, [nc.scalar] * 4)
         ident = sb.tile([P, P], F32, name="ident")
         make_identity(nc, ident[:])
         placed = sb.tile([P, T], F32, name="placed")
         nc.vector.memset(placed[:], 0.0)
 
+        warm = sb.tile([P, 1], F32, name="warm")
+        nc.scalar.activation(warm[:], placed[:, 0:1], ACT.Exp)
+        q_bf = early.tile([P, Q, PACK], BF16, name="q_bf", offset=1984, align_bytes=64)
+        round_rows(q_raw, q_bf)
+        dq_raw = stage.tile([P, PACK, Q], F32, name="dq_raw", offset=0)
+        load_rows(dquery, dq_raw)
+        val_pool = stage.tile([P, T], U32, name="val_pool", offset=4032)
+        load_words(vals_words, val_pool)
+        q_codes, q_scales = quantize(q_bf, "q")
+        go_raw = early.tile([P, PACK, Q], F32, name="go_raw", offset=0, align_bytes=64)
+        load_rows(gout, go_raw)
+        val_scale_pool = early.tile([P, T], U8, name="val_scale_pool", offset=2944, align_bytes=64)
+        nc.vector.memset(val_scale_pool[:].bitcast(I32), 0)
+        load_scale_rows(val_scale_pool, vals_scales, VAL_PLANE, [nc.scalar] * 4)
         key_scales = sb.tile([P, I], U8, name="key_scales", align_bytes=64)
         nc.vector.tensor_copy(key_scales[:], key_scale_pool[:].indirect(offsets[:]))
-        q_bf = round_rows(q_raw, "q_bf")
-        warm = sb.tile([P, 1], F32, name="warm")
-        nc.scalar.activation(warm[:], q_bf[:, 0, 0:1], ACT.Exp, scale=0.0)
-        dq_raw = load_rows(dquery, "dq_raw")
-        val_pool = load_words(vals_words, "val_pool", "second")
-        q_codes, q_scales = quantize(q_bf, "q")
-        size_cols = sb.tile([P, I // P], F32, name="size_cols", tag="q_bf", align_bytes=64)
-        with nc.allow_non_contiguous_dma(reason="one weight a partition"):
-            nc.sync.dma_start(out=size_cols[:], in_=size[0].rearrange("(t p) -> p t", p=P))
-        val_scales = sb.tile([P, I], U8, name="val_scales", align_bytes=64)
-        nc.vector.tensor_copy(val_scales[:], val_scale_pool[:].indirect(offsets[:]))
 
         neg_slope = sb.tile([P, 1], F32, name="neg_slope")
         slope = sb.tile([P, 1], F32, name="slope")
         shift = sb.tile([P, 1], F32, name="shift")
         c_scale = sb.tile([P, I // P], F32, name="c_scale")
-        nc.gpsimd.tensor_scalar(neg_slope[:], steep_col[:], -1.0 / PAGE, 0.0, ALU.mult, ALU.add)
-        nc.gpsimd.tensor_scalar(slope[:], steep_col[:], 1.0 / PAGE, 0.0, ALU.mult, ALU.add)
-        nc.gpsimd.tensor_tensor(shift[:], steep_col[:], th_col[:], ALU.mult)
-        nc.gpsimd.tensor_scalar(c_scale[:], size_cols[:], -512.0, 0.0, ALU.mult, ALU.add)
 
         halves = [slice(h * HALF, (h + 1) * HALF) for h in range(2)]
         page_halves = [slice(h * G // 2, (h + 1) * G // 2) for h in range(2)]
@@ -122,8 +116,15 @@ def tile_attend_hvpagegate_s_kernel(tc, query, keys_words, keys_scales, th, stee
             nc.tensor.matmul_mx(out=a_ps[h][:], lhsT=q_codes[:].bitcast(FP8X4), lhsT_scale=q_scales[:],
                                 rhs=key_words[:, halves[h]].bitcast(FP8X4), rhs_scale=key_scales[:, halves[h]],
                                 start=True, stop=True)
-        dq_bf = round_rows(dq_raw, "dq_bf")
-        go_raw = load_rows(gout, "go_raw")
+        nc.vector.tensor_scalar(neg_slope[:], steep_col[:], -1.0 / PAGE, None, ALU.mult)
+        nc.vector.tensor_scalar(slope[:], steep_col[:], 1.0 / PAGE, None, ALU.mult)
+        nc.vector.tensor_tensor(shift[:], steep_col[:], th_col[:], ALU.mult)
+        dq_bf = sb.tile([P, Q, PACK], BF16, name="dq_bf", align_bytes=64)
+        round_rows(dq_raw, dq_bf)
+        size_cols = stage.tile([P, I // P], F32, name="size_cols", offset=0)
+        with nc.allow_non_contiguous_dma(reason="one weight a partition"):
+            nc.sync.dma_start(out=size_cols[:], in_=size[0].rearrange("(t p) -> p t", p=P))
+        nc.gpsimd.tensor_scalar(c_scale[:], size_cols[:], -512.0, 0.0, ALU.mult, ALU.add)
 
         a_sum = sb.tile([P, G], F32, name="a_sum")
         a_max = sb.tile([P, 2], F32, name="a_max")
@@ -144,12 +145,15 @@ def tile_attend_hvpagegate_s_kernel(tc, query, keys_words, keys_scales, th, stee
         r = sb.tile([P, I], F32, name="r")
         for h in range(2):
             nc.scalar.activation(r[:, halves[h]], a_ps[h][:], ACT.Exp, bias=neg_max[:])
-        go_bf = round_rows(go_raw, "go_bf")
+        go_bf = sb.tile([P, Q, PACK], BF16, name="go_bf", align_bytes=64)
+        round_rows(go_raw, go_bf)
 
+        val_scales = sb.tile([P, I], U8, name="val_scales", align_bytes=64)
+        nc.vector.tensor_copy(val_scales[:], val_scale_pool[:].indirect(offsets[:]))
         val_words = sb.tile([P, I], U32, name="val_words", align_bytes=64)
         nc.vector.tensor_copy(val_words[:], val_pool[:].indirect(offsets[:]))
         go_codes, go_scales = quantize(go_bf, "go")
-        base_sb = sb.tile([P, T], F32, name="base_sb", tag="second")
+        base_sb = stage.tile([P, T], F32, name="base_sb", offset=4288)
         nc.sync.dma_start(out=base_sb[:], in_=base)
         ct_ps = [ps.tile([P, 2, Q], F32, name="ct_ps%d" % h) for h in range(2)]
         ct = sb.tile([P, I // P, Q], F32, name="ct")
@@ -164,8 +168,8 @@ def tile_attend_hvpagegate_s_kernel(tc, query, keys_words, keys_scales, th, stee
         for t in range(I // P):
             nc.tensor.transpose(c_ps[:, t * P:(t + 1) * P], ct[:, t, :], ident[:])
 
-        gate = sb.tile([P, G], F32, name="gate")
-        ta_sum = sb.tile([P, G], F32, name="ta_sum")
+        gate = stage.tile([P, G], F32, name="gate", offset=4032)
+        ta_sum = stage.tile([P, G], F32, name="ta_sum", offset=4160)
         k_m = sb.tile([P, G], F32, name="k_m")
         lift = sb.tile([P, G], F32, name="lift")
         k_n = sb.tile([P, G], F32, name="k_n")
@@ -191,35 +195,33 @@ def tile_attend_hvpagegate_s_kernel(tc, query, keys_words, keys_scales, th, stee
         nc.vector.scalar_tensor_tensor(terms[:], c_ps[:], inv_z[:], p[:], ALU.mult, ALU.mult, accum_out=c_mean[:])
         nc.vector.scalar_tensor_tensor(terms2[:], w[:], inv_z[:], p[:], ALU.mult, ALU.mult, accum_out=w_mean[:])
         u = sb.tile([P, I], F32, name="u")
-        nc.vector.scalar_tensor_tensor(u[:], c_ps[:], c_mean[:], prob[:], ALU.subtract, ALU.mult)
+        for h in range(2):
+            nc.vector.scalar_tensor_tensor(u[:, halves[h]], c_ps[:, halves[h]], c_mean[:], prob[:, halves[h]],
+                                           ALU.subtract, ALU.mult)
         v = sb.tile([P, I], F32, name="v")
         cov = sb.tile([P, 1], F32, name="cov")
-        nc.vector.scalar_tensor_tensor(v[:], w[:], w_mean[:], u[:], ALU.subtract, ALU.mult, accum_out=cov[:])
         u_sum = sb.tile([P, G], F32, name="u_sum")
-        nc.vector.tensor_reduce(u_sum[:], paged(u[:]), AX.X, ALU.add)
-        m = [sb.tile([P, HALF], F32, name="m%d" % h) for h in range(2)]
-        m_sum = [sb.tile([P, G // 2], F32, name="m_sum%d" % h) for h in range(2)]
+        nc.vector.tensor_reduce(u_sum[:, page_halves[0]], paged(u[:, halves[0]]), AX.X, ALU.add)
+        nc.vector.scalar_tensor_tensor(v[:], w[:], w_mean[:], u[:], ALU.subtract, ALU.mult, accum_out=cov[:])
+        nc.vector.tensor_reduce(u_sum[:, page_halves[1]], paged(u[:, halves[1]]), AX.X, ALU.add)
+        m = sb.tile([P, I], F32, name="m")
+        m_sum = sb.tile([P, G], F32, name="m_sum")
         n_term = sb.tile([P, G], F32, name="n_term")
         for h in range(2):
-            nc.vector.scalar_tensor_tensor(m[h][:], prob[:, halves[h]], cov[:], v[:, halves[h]], ALU.mult,
+            nc.vector.scalar_tensor_tensor(m[:, halves[h]], prob[:, halves[h]], cov[:], v[:, halves[h]], ALU.mult,
                                            ALU.subtract)
         nc.vector.tensor_tensor(n_term[:], u_sum[:], k_n[:], ALU.mult)
         for h in range(2):
-            nc.vector.tensor_reduce(m_sum[h][:], paged(m[h][:]), AX.X, ALU.add)
-        pages = G // SCATTERS
-        for s in range(SCATTERS):
-            spread = sb.tile([P, pages, PAGE], F32, name="spread%d" % s)
-            h, first = divmod(s * pages, G // 2)
-            for j in range(pages):
-                g = s * pages + j
-                nc.scalar.activation(spread[:, j, :], m_sum[h][:, first + j:first + j + 1].to_broadcast([P, PAGE]),
+            nc.vector.tensor_reduce(m_sum[:, page_halves[h]], paged(m[:, halves[h]]), AX.X, ALU.add)
+        spread = sb.tile([P, I], F32, name="spread")
+        for first, last in SCATTERS:
+            for g in range(first, last):
+                nc.scalar.activation(spread[:, g * PAGE:(g + 1) * PAGE], m_sum[:, g:g + 1].to_broadcast([P, PAGE]),
                                      ACT.Identity, bias=n_term[:, g:g + 1], scale=k_m[:, g:g + 1])
-            nc.vector.tensor_tensor(placed[:].indirect(offsets[:, s * pages:(s + 1) * pages]),
-                                    m[h][:, first * PAGE:(first + pages) * PAGE],
-                                    spread[:].rearrange("p g j -> p (g j)"), ALU.add)
-        width = T // STORES
-        for s in range(STORES):
-            cols = slice(s * width, (s + 1) * width)
+            cols = slice(first * PAGE, last * PAGE)
+            nc.vector.tensor_tensor(placed[:].indirect(offsets[:, first:last]), m[:, cols], spread[:, cols], ALU.add)
+        for s, width in enumerate(STORES):
+            cols = slice(sum(STORES[:s]), sum(STORES[:s + 1]))
             res = sb.tile([P, width], F32, name="res%d" % s)
             nc.vector.tensor_tensor(res[:], placed[:, cols], base_sb[:, cols], ALU.add)
             nc.sync.dma_start(out=out[:, cols], in_=res[:])

@@ -69,47 +69,49 @@ def tile_attend_hvpagegate_s_kernel(tc, query, keys_words, keys_scales, th, stee
                 queue.dma_start(out=window[row:row + 4, :].bitcast(I32),
                                 in_=scales[0, 4 * quad:4 * quad + 4, :].bitcast(I32))
 
-        key_scale_pool = sb.tile([P, T], U8, name="key_scale_pool")
+        key_scale_pool = sb.tile([P, T], U8, name="key_scale_pool", tag="key_scale_pool", align_bytes=64)
         q_raw = stage.tile([P, PACK, Q], F32, name="q_raw", offset=2016)
         load_rows(query, q_raw)
-        th_col = sb.tile([P, 1], F32, name="th_col")
-        steep_col = sb.tile([P, 1], F32, name="steep_col")
-        nc.sync.dma_start(out=steep_col[:], in_=steep)
-        nc.sync.dma_start(out=th_col[:], in_=th)
         key_pool = sb.tile([P, T], U32, name="key_pool")
         load_words(keys_words, key_pool)
         nc.gpsimd.memset(key_scale_pool[:].bitcast(I32), 0)
         load_scale_rows(key_scale_pool, keys_scales, 0, [nc.scalar] * 4)
+        warm_in = sb.tile([P, 1], F32, name="warm_in")
+        nc.gpsimd.memset(warm_in[:], 0.0)
         ident = sb.tile([P, P], F32, name="ident")
         make_identity(nc, ident[:])
         placed = sb.tile([P, T], F32, name="placed")
         nc.vector.memset(placed[:], 0.0)
 
         warm = sb.tile([P, 1], F32, name="warm")
-        nc.scalar.activation(warm[:], placed[:, 0:1], ACT.Exp)
-        q_bf = early.tile([P, Q, PACK], BF16, name="q_bf", offset=1984, align_bytes=64)
+        nc.scalar.activation(warm[:], warm_in[:], ACT.Exp)
+        q_bf = early.tile([P, Q, PACK], BF16, name="q_bf", offset=8128, align_bytes=64)
         round_rows(q_raw, q_bf)
         dq_raw = stage.tile([P, PACK, Q], F32, name="dq_raw", offset=0)
         load_rows(dquery, dq_raw)
-        val_pool = stage.tile([P, T], U32, name="val_pool", offset=4032)
-        load_words(vals_words, val_pool)
-        q_codes, q_scales = quantize(q_bf, "q")
-        go_raw = early.tile([P, PACK, Q], F32, name="go_raw", offset=0, align_bytes=64)
+        go_raw = stage.tile([P, PACK, Q], F32, name="go_raw", offset=4032)
         load_rows(gout, go_raw)
-        val_scale_pool = early.tile([P, T], U8, name="val_scale_pool", offset=2944, align_bytes=64)
+        q_codes, q_scales = quantize(q_bf, "q")
+        val_pool = early.tile([P, T], U32, name="val_pool", offset=0, align_bytes=64)
+        load_words(vals_words, val_pool)
+        steep_col = early.tile([P, 1], F32, name="steep_col", offset=8448, align_bytes=64)
+        th_col = early.tile([P, 1], F32, name="th_col", offset=8512, align_bytes=64)
+        nc.scalar.dma_start(out=steep_col[:], in_=steep)
+        nc.scalar.dma_start(out=th_col[:], in_=th)
+        val_scale_pool = early.tile([P, T], U8, name="val_scale_pool", offset=9088, align_bytes=64)
         nc.vector.memset(val_scale_pool[:].bitcast(I32), 0)
         load_scale_rows(val_scale_pool, vals_scales, VAL_PLANE, [nc.scalar] * 4)
-        key_scales = sb.tile([P, I], U8, name="key_scales", align_bytes=64)
+        key_scales = early.tile([P, I], U8, name="key_scales", offset=8576, align_bytes=64)
         nc.vector.tensor_copy(key_scales[:], key_scale_pool[:].indirect(offsets[:]))
 
         neg_slope = sb.tile([P, 1], F32, name="neg_slope")
         slope = sb.tile([P, 1], F32, name="slope")
         shift = sb.tile([P, 1], F32, name="shift")
-        c_scale = sb.tile([P, I // P], F32, name="c_scale")
+        c_scale = sb.tile([P, I // P], F32, name="c_scale", tag="c_scale")
 
         halves = [slice(h * HALF, (h + 1) * HALF) for h in range(2)]
         page_halves = [slice(h * G // 2, (h + 1) * G // 2) for h in range(2)]
-        key_words = sb.tile([P, I], U32, name="key_words", align_bytes=64)
+        key_words = sb.tile([P, I], U32, name="key_words", tag="key_scale_pool", align_bytes=64)
         a_ps = [ps.tile([P, HALF], F32, name="a_ps%d" % h) for h in range(2)]
         for h in range(2):
             nc.vector.tensor_copy(key_words[:, halves[h]], key_pool[:].indirect(offsets[:, page_halves[h]]))
@@ -121,6 +123,8 @@ def tile_attend_hvpagegate_s_kernel(tc, query, keys_words, keys_scales, th, stee
         nc.vector.tensor_tensor(shift[:], steep_col[:], th_col[:], ALU.mult)
         dq_bf = sb.tile([P, Q, PACK], BF16, name="dq_bf", align_bytes=64)
         round_rows(dq_raw, dq_bf)
+        go_bf = sb.tile([P, Q, PACK], BF16, name="go_bf", tag="go_bf", align_bytes=64)
+        round_rows(go_raw, go_bf)
         size_cols = stage.tile([P, I // P], F32, name="size_cols", offset=0)
         with nc.allow_non_contiguous_dma(reason="one weight a partition"):
             nc.sync.dma_start(out=size_cols[:], in_=size[0].rearrange("(t p) -> p t", p=P))
@@ -138,22 +142,20 @@ def tile_attend_hvpagegate_s_kernel(tc, query, keys_words, keys_scales, th, stee
         nc.tensor.matmul_mx(out=ta_ps[:], lhsT=dq_codes[:].bitcast(FP8X4), lhsT_scale=dq_scales[:],
                             rhs=key_words[:].bitcast(FP8X4), rhs_scale=key_scales[:], start=True, stop=True)
 
-        odds = sb.tile([P, G], F32, name="odds")
+        odds = stage.tile([P, G], F32, name="odds", offset=4032)
         denom = sb.tile([P, G], F32, name="denom")
         nc.scalar.activation(odds[:], a_sum[:], ACT.Exp, bias=shift[:], scale=neg_slope[:])
         nc.scalar.activation(denom[:], odds[:], ACT.Identity, bias=1.0)
-        r = sb.tile([P, I], F32, name="r")
+        r = stage.tile([P, I], F32, name="r", offset=4160)
         for h in range(2):
             nc.scalar.activation(r[:, halves[h]], a_ps[h][:], ACT.Exp, bias=neg_max[:])
-        go_bf = sb.tile([P, Q, PACK], BF16, name="go_bf", align_bytes=64)
-        round_rows(go_raw, go_bf)
 
         val_scales = sb.tile([P, I], U8, name="val_scales", align_bytes=64)
         nc.vector.tensor_copy(val_scales[:], val_scale_pool[:].indirect(offsets[:]))
-        val_words = sb.tile([P, I], U32, name="val_words", align_bytes=64)
-        nc.vector.tensor_copy(val_words[:], val_pool[:].indirect(offsets[:]))
         go_codes, go_scales = quantize(go_bf, "go")
-        base_sb = stage.tile([P, T], F32, name="base_sb", offset=4288)
+        val_words = sb.tile([P, I], U32, name="val_words", tag="go_bf", align_bytes=64)
+        nc.vector.tensor_copy(val_words[:], val_pool[:].indirect(offsets[:]))
+        base_sb = early.tile([P, T], F32, name="base_sb", offset=256, align_bytes=64)
         nc.sync.dma_start(out=base_sb[:], in_=base)
         ct_ps = [ps.tile([P, 2, Q], F32, name="ct_ps%d" % h) for h in range(2)]
         ct = sb.tile([P, I // P, Q], F32, name="ct")
@@ -168,8 +170,8 @@ def tile_attend_hvpagegate_s_kernel(tc, query, keys_words, keys_scales, th, stee
         for t in range(I // P):
             nc.tensor.transpose(c_ps[:, t * P:(t + 1) * P], ct[:, t, :], ident[:])
 
-        gate = stage.tile([P, G], F32, name="gate", offset=4032)
-        ta_sum = stage.tile([P, G], F32, name="ta_sum", offset=4160)
+        gate = early.tile([P, G], F32, name="gate", offset=0, align_bytes=64)
+        ta_sum = early.tile([P, G], F32, name="ta_sum", offset=128, align_bytes=64)
         k_m = sb.tile([P, G], F32, name="k_m")
         lift = sb.tile([P, G], F32, name="lift")
         k_n = sb.tile([P, G], F32, name="k_n")
@@ -185,7 +187,7 @@ def tile_attend_hvpagegate_s_kernel(tc, query, keys_words, keys_scales, th, stee
         nc.vector.reciprocal(inv_z[:], z[:])
         w = sb.tile([P, I], F32, name="w")
         nc.vector.tensor_tensor(paged(w[:]), paged(ta_ps[:]), over_page(lift[:]), ALU.add)
-        prob = sb.tile([P, I], F32, name="prob")
+        prob = sb.tile([P, I], F32, name="prob", tag="c_scale")
         nc.scalar.activation(prob[:], p[:], ACT.Copy, scale=inv_z[:])
         nc.vector.scalar_tensor_tensor(k_n[:], lift[:], slope[:], gate[:], ALU.mult, ALU.mult)
         terms = sb.tile([P, I], F32, name="terms")

from contextlib import ExitStack

import concourse.mybir as mybir
from concourse.masks import make_identity

D, E, T, I, Q, G = 512, 512, 2048, 512, 128, 32
P = 128
PACK = 4
PAGE = I // G
HALF = I // 2
FLOPS = 3 * 2 * D * Q * I

F32 = mybir.dt.float32
BF16 = mybir.dt.bfloat16
I32 = mybir.dt.int32
U32 = mybir.dt.uint32
U16 = mybir.dt.uint16
U8 = mybir.dt.uint8
FP8X4 = mybir.dt.float8_e4m3fn_x4
ALU = mybir.AluOpType
ACT = mybir.ActivationFunctionType
AX = mybir.AxisListType

VAL_PLANE = 4
SCATTERS = ((0, 8), (8, 16), (16, 32))
STORES = (256, 512, 512, 512, 256)


def paged(ap):
    return ap.rearrange("p (g j) -> p g j", j=PAGE)


def over_page(ap):
    return ap.unsqueeze(2).to_broadcast([P, ap.shape[1], PAGE])


def tile_attend_hvpagegate_s_kernel(tc, query, keys_words, keys_scales, th, steep, gout, vals_words, vals_scales,
                                     size, dquery, base, offs, out):
    nc = tc.nc
    with ExitStack() as ctx:
        held = ctx.enter_context(tc.tile_pool(name="held", bufs=1))
        sb = ctx.enter_context(tc.tile_pool(name="sb", bufs=1))
        stage = ctx.enter_context(tc.tile_pool(name="stage", bufs=1))
        early = ctx.enter_context(tc.tile_pool(name="early", bufs=1))
        ps = ctx.enter_context(tc.psum_pool(name="ps", bufs=1))

        offsets = held.tile([P, I // 16], U16, name="offsets")
        nc.sync.dma_start(offsets[:], offs)

        def load_rows(src, raw):
            nc.sync.dma_start(out=raw[:], in_=src.rearrange("(p j) w -> p j w", j=PACK))

        def round_rows(raw, grouped):
            nc.scalar.copy(out=grouped[:], in_=raw[:].rearrange("p j w -> p w j"))

        def quantize(grouped, name):
            codes = sb.tile([P, Q], U32, name=name + "_codes", align_bytes=64)
            scales = sb.tile([P, Q], U8, name=name + "_scales", align_bytes=64)
            nc.vector.quantize_mx(out=codes[:].bitcast(FP8X4), scales=scales[:],
                                  in_=grouped[:].rearrange("p w j -> p (w j)"))
            return codes, scales

        def load_words(words, window):
            nc.sync.dma_start(out=window[:].bitcast(I32), in_=words[0].rearrange("p n t -> p (n t)").bitcast(I32))

        def load_scale_rows(window, scales, first, queues):
            for quad, queue in enumerate(queues):
                row = 32 * quad + first
                queue.dma_start(out=window[row:row + 4, :].bitcast(I32),
                                in_=scales[0, 4 * quad:4 * quad + 4, :].bitcast(I32))

        key_scale_pool = sb.tile([P, T], U8, name="key_scale_pool", tag="key_scale_pool", align_bytes=64)
        q_raw = stage.tile([P, PACK, Q], F32, name="q_raw", offset=2016)
        load_rows(query, q_raw)
        key_pool = sb.tile([P, T], U32, name="key_pool")
        load_words(keys_words, key_pool)
        nc.gpsimd.memset(key_scale_pool[:].bitcast(I32), 0)
        load_scale_rows(key_scale_pool, keys_scales, 0, [nc.scalar] * 4)
        warm_in = sb.tile([P, 1], F32, name="warm_in")
        nc.gpsimd.memset(warm_in[:], 0.0)
        ident = sb.tile([P, P], F32, name="ident")
        make_identity(nc, ident[:])
        placed = sb.tile([P, T], F32, name="placed")
        nc.vector.memset(placed[:], 0.0)

        warm = sb.tile([P, 1], F32, name="warm")
        nc.scalar.activation(warm[:], warm_in[:], ACT.Exp)
        q_bf = early.tile([P, Q, PACK], BF16, name="q_bf", offset=8128, align_bytes=64)
        round_rows(q_raw, q_bf)
        dq_raw = stage.tile([P, PACK, Q], F32, name="dq_raw", offset=0)
        load_rows(dquery, dq_raw)
        go_raw = stage.tile([P, PACK, Q], F32, name="go_raw", offset=4032)
        load_rows(gout, go_raw)
        q_codes, q_scales = quantize(q_bf, "q")
        val_pool = early.tile([P, T], U32, name="val_pool", offset=0, align_bytes=64)
        load_words(vals_words, val_pool)
        steep_col = early.tile([P, 1], F32, name="steep_col", offset=8448, align_bytes=64)
        th_col = early.tile([P, 1], F32, name="th_col", offset=8512, align_bytes=64)
        nc.scalar.dma_start(out=steep_col[:], in_=steep)
        nc.scalar.dma_start(out=th_col[:], in_=th)
        val_scale_pool = early.tile([P, T], U8, name="val_scale_pool", offset=9088, align_bytes=64)
        nc.vector.memset(val_scale_pool[:].bitcast(I32), 0)
        load_scale_rows(val_scale_pool, vals_scales, VAL_PLANE, [nc.scalar] * 4)
        key_scales = early.tile([P, I], U8, name="key_scales", offset=8576, align_bytes=64)
        nc.vector.tensor_copy(key_scales[:], key_scale_pool[:].indirect(offsets[:]))

        neg_slope = sb.tile([P, 1], F32, name="neg_slope")
        slope = sb.tile([P, 1], F32, name="slope")
        shift = sb.tile([P, 1], F32, name="shift")
        c_scale = sb.tile([P, I // P], F32, name="c_scale", tag="c_scale")

        halves = [slice(h * HALF, (h + 1) * HALF) for h in range(2)]
        page_halves = [slice(h * G // 2, (h + 1) * G // 2) for h in range(2)]
        key_words = sb.tile([P, I], U32, name="key_words", tag="key_scale_pool", align_bytes=64)
        a_ps = [ps.tile([P, HALF], F32, name="a_ps%d" % h) for h in range(2)]
        for h in range(2):
            nc.vector.tensor_copy(key_words[:, halves[h]], key_pool[:].indirect(offsets[:, page_halves[h]]))
            nc.tensor.matmul_mx(out=a_ps[h][:], lhsT=q_codes[:].bitcast(FP8X4), lhsT_scale=q_scales[:],
                                rhs=key_words[:, halves[h]].bitcast(FP8X4), rhs_scale=key_scales[:, halves[h]],
                                start=True, stop=True)
        nc.vector.tensor_scalar(neg_slope[:], steep_col[:], -1.0 / PAGE, None, ALU.mult)
        nc.vector.tensor_scalar(slope[:], steep_col[:], 1.0 / PAGE, None, ALU.mult)
        nc.vector.tensor_tensor(shift[:], steep_col[:], th_col[:], ALU.mult)
        dq_bf = sb.tile([P, Q, PACK], BF16, name="dq_bf", align_bytes=64)
        round_rows(dq_raw, dq_bf)
        go_bf = sb.tile([P, Q, PACK], BF16, name="go_bf", tag="go_bf", align_bytes=64)
        round_rows(go_raw, go_bf)
        size_cols = stage.tile([P, I // P], F32, name="size_cols", offset=0)
        with nc.allow_non_contiguous_dma(reason="one weight a partition"):
            nc.sync.dma_start(out=size_cols[:], in_=size[0].rearrange("(t p) -> p t", p=P))
        nc.gpsimd.tensor_scalar(c_scale[:], size_cols[:], -512.0, 0.0, ALU.mult, ALU.add)

        a_sum = sb.tile([P, G], F32, name="a_sum")
        a_max = sb.tile([P, 2], F32, name="a_max")
        neg_max = sb.tile([P, 1], F32, name="neg_max")
        for h in range(2):
            nc.vector.tensor_reduce(a_sum[:, page_halves[h]], paged(a_ps[h][:]), AX.X, ALU.add)
            nc.vector.tensor_reduce(a_max[:, h:h + 1], a_ps[h][:], AX.X, ALU.max)
        dq_codes, dq_scales = quantize(dq_bf, "dq")
        nc.vector.tensor_reduce(neg_max[:], a_max[:], AX.X, ALU.max, negate=True)
        ta_ps = ps.tile([P, I], F32, name="ta_ps")
        nc.tensor.matmul_mx(out=ta_ps[:], lhsT=dq_codes[:].bitcast(FP8X4), lhsT_scale=dq_scales[:],
                            rhs=key_words[:].bitcast(FP8X4), rhs_scale=key_scales[:], start=True, stop=True)

        odds = stage.tile([P, G], F32, name="odds", offset=4032)
        denom = sb.tile([P, G], F32, name="denom")
        nc.scalar.activation(odds[:], a_sum[:], ACT.Exp, bias=shift[:], scale=neg_slope[:])
        nc.scalar.activation(denom[:], odds[:], ACT.Identity, bias=1.0)
        r = stage.tile([P, I], F32, name="r", offset=4160)
        for h in range(2):
            nc.scalar.activation(r[:, halves[h]], a_ps[h][:], ACT.Exp, bias=neg_max[:])

        val_scales = sb.tile([P, I], U8, name="val_scales", align_bytes=64)
        nc.vector.tensor_copy(val_scales[:], val_scale_pool[:].indirect(offsets[:]))
        go_codes, go_scales = quantize(go_bf, "go")
        val_words = sb.tile([P, I], U32, name="val_words", tag="go_bf", align_bytes=64)
        nc.vector.tensor_copy(val_words[:], val_pool[:].indirect(offsets[:]))
        base_sb = early.tile([P, T], F32, name="base_sb", offset=256, align_bytes=64)
        nc.sync.dma_start(out=base_sb[:], in_=base)
        ct_ps = [ps.tile([P, 2, Q], F32, name="ct_ps%d" % h) for h in range(2)]
        ct = sb.tile([P, I // P, Q], F32, name="ct")
        c_ps = ps.tile([P, I], F32, name="c_ps")
        for t in range(I // P):
            cols = slice(t * P, (t + 1) * P)
            nc.tensor.matmul_mx(out=ct_ps[t // 2][:, t % 2, :], lhsT=val_words[:, cols].bitcast(FP8X4),
                                lhsT_scale=val_scales[VAL_PLANE:P, cols], rhs=go_codes[:].bitcast(FP8X4),
                                rhs_scale=go_scales[:], start=True, stop=True)
        for t in range(I // P):
            nc.scalar.activation(ct[:, t, :], ct_ps[t // 2][:, t % 2, :], ACT.Copy, scale=c_scale[:, t:t + 1])
        for t in range(I // P):
            nc.tensor.transpose(c_ps[:, t * P:(t + 1) * P], ct[:, t, :], ident[:])

        gate = early.tile([P, G], F32, name="gate", offset=0, align_bytes=64)
        ta_sum = early.tile([P, G], F32, name="ta_sum", offset=128, align_bytes=64)
        k_m = sb.tile([P, G], F32, name="k_m")
        lift = sb.tile([P, G], F32, name="lift")
        k_n = sb.tile([P, G], F32, name="k_n")
        nc.vector.reciprocal(gate[:], denom[:])
        nc.vector.tensor_reduce(ta_sum[:], paged(ta_ps[:]), AX.X, ALU.add)
        nc.vector.tensor_scalar(k_m[:], gate[:], 1.0, neg_slope[:], ALU.subtract, ALU.mult)
        p = sb.tile([P, I], F32, name="p")
        z = sb.tile([P, 1], F32, name="z")
        nc.vector.scalar_tensor_tensor(paged(p[:]), paged(r[:]), 1.0, over_page(gate[:]), ALU.mult, ALU.mult,
                                       accum_out=z[:])
        nc.vector.tensor_tensor(lift[:], ta_sum[:], k_m[:], ALU.mult)
        inv_z = sb.tile([P, 1], F32, name="inv_z")
        nc.vector.reciprocal(inv_z[:], z[:])
        w = sb.tile([P, I], F32, name="w")
        nc.vector.tensor_tensor(paged(w[:]), paged(ta_ps[:]), over_page(lift[:]), ALU.add)
        prob = sb.tile([P, I], F32, name="prob", tag="c_scale")
        nc.scalar.activation(prob[:], p[:], ACT.Copy, scale=inv_z[:])
        nc.vector.scalar_tensor_tensor(k_n[:], lift[:], slope[:], gate[:], ALU.mult, ALU.mult)
        terms = sb.tile([P, I], F32, name="terms")
        terms2 = sb.tile([P, I], F32, name="terms2")
        c_mean = sb.tile([P, 1], F32, name="c_mean")
        w_mean = sb.tile([P, 1], F32, name="w_mean")
        nc.vector.scalar_tensor_tensor(terms[:], c_ps[:], inv_z[:], p[:], ALU.mult, ALU.mult, accum_out=c_mean[:])
        nc.vector.scalar_tensor_tensor(terms2[:], w[:], inv_z[:], p[:], ALU.mult, ALU.mult, accum_out=w_mean[:])
        u = sb.tile([P, I], F32, name="u")
        for h in range(2):
            nc.vector.scalar_tensor_tensor(u[:, halves[h]], c_ps[:, halves[h]], c_mean[:], prob[:, halves[h]],
                                           ALU.subtract, ALU.mult)
        v = sb.tile([P, I], F32, name="v")
        cov = sb.tile([P, 1], F32, name="cov")
        u_sum = sb.tile([P, G], F32, name="u_sum")
        nc.vector.tensor_reduce(u_sum[:, page_halves[0]], paged(u[:, halves[0]]), AX.X, ALU.add)
        nc.vector.scalar_tensor_tensor(v[:], w[:], w_mean[:], u[:], ALU.subtract, ALU.mult, accum_out=cov[:])
        nc.vector.tensor_reduce(u_sum[:, page_halves[1]], paged(u[:, halves[1]]), AX.X, ALU.add)
        m = sb.tile([P, I], F32, name="m")
        m_sum = sb.tile([P, G], F32, name="m_sum")
        n_term = sb.tile([P, G], F32, name="n_term")
        for h in range(2):
            nc.vector.scalar_tensor_tensor(m[:, halves[h]], prob[:, halves[h]], cov[:], v[:, halves[h]], ALU.mult,
                                           ALU.subtract)
        nc.vector.tensor_tensor(n_term[:], u_sum[:], k_n[:], ALU.mult)
        for h in range(2):
            nc.vector.tensor_reduce(m_sum[:, page_halves[h]], paged(m[:, halves[h]]), AX.X, ALU.add)
        spread = sb.tile([P, I], F32, name="spread")
        for first, last in SCATTERS:
            for g in range(first, last):
                nc.scalar.activation(spread[:, g * PAGE:(g + 1) * PAGE], m_sum[:, g:g + 1].to_broadcast([P, PAGE]),
                                     ACT.Identity, bias=n_term[:, g:g + 1], scale=k_m[:, g:g + 1])
            cols = slice(first * PAGE, last * PAGE)
            nc.vector.tensor_tensor(placed[:].indirect(offsets[:, first:last]), m[:, cols], spread[:, cols], ALU.add)
        for s, width in enumerate(STORES):
            cols = slice(sum(STORES[:s]), sum(STORES[:s + 1]))
            res = sb.tile([P, width], F32, name="res%d" % s)
            nc.vector.tensor_tensor(res[:], placed[:, cols], base_sb[:, cols], ALU.add)
            nc.sync.dma_start(out=out[:, cols], in_=res[:])
